import numpy as np, ml_dtypes
CORES = [24,40,56,80,88,96]
N = 6
WB, F = 2, 512
def setup_inputs(rng):
    return {"a": rng.standard_normal((N, 128, 128), dtype=np.float32).astype(ml_dtypes.bfloat16), "w": rng.standard_normal((N, 128, F), dtype=np.float32).astype(ml_dtypes.bfloat16)}
def setup_inputs_big(rng):
    d = setup_inputs(rng)
    for k in ("a", "w"): d[k] = (d[k].astype(np.float32) * 1024.0).astype(d[k].dtype)
    return d
def setup_inputs_small(rng):
    d = setup_inputs(rng)
    for k in ("a", "w"): d[k] = (d[k].astype(np.float32) * (1 / 1024.0)).astype(d[k].dtype)
    return d
def setup_inputs_apart(rng):
    d = setup_inputs(rng)
    f = (10.0 ** rng.permutation(np.linspace(-1.5, 1.5, N))).astype(np.float32).reshape(N, 1, 1)
    for k in ("a", "w"): d[k] = (d[k].astype(np.float32) * f).astype(d[k].dtype)
    return d
def reference(a, w):
    A, W = a.astype(np.float64), w.astype(np.float64)
    p = [A[j].T @ W[j] for j in range(N)]
    y = np.stack([sum(p[(r - i) % N] for i in range(WB + 1)) for r in range(N)])
    return {"y": y.astype(ml_dtypes.bfloat16 if a.dtype != np.float64 else np.float64)}

@@ -1,0 +1,138 @@
+from concourse.bass import DstId, RemoteDMATransfer
+from concourse.mybir import AluOpType
+
+F = 512
+NE = 8
+
+SCRATCH = {
+    "asb": ("sbuf", [128, 128], "bfloat16"),
+    "wsb": ("sbuf", [128, F], "bfloat16"),
+    "ps": ("psum", [128, F], "float32"),
+    "acc": ("psum", [128, F], "float32"),
+    "pb": ("sbuf", [128, F], "bfloat16"),
+    "in0": ("sbuf", [128, F], "bfloat16"),
+    "in1": ("sbuf", [128, F], "bfloat16"),
+    "out": ("sbuf", [128, F], "bfloat16"),
+}
+SEMAPHORES = ["loaded", "mm", "cp", "arr0", "arr1", "vs", "fin", "stored", "sent"]
+
+
+def _engines(mask, k, avoid=0):
+    got, n = 0, 0
+    for b in reversed(range(mask.bit_length())):
+        bit = 1 << b
+        if (mask & bit) and not (avoid & bit) and n < k:
+            got |= bit
+            n += 1
+    return got
+
+
+def _plan(T, topo):
+    cores = list(T.cores)
+    n = len(cores)
+    busy = set(cores)
+    first, then, slots = {}, {}, {}
+
+    def job(book, src, bufs, dst, slot):
+        book.setdefault(src, []).append((bufs, dst, slot))
+        slots.setdefault(dst, []).append(slot)
+
+    def relay(home, feeders, dst):
+        for same_die in (True, False):
+            for c in range(topo.CORES_PER_CHIP * topo.CHIPS):
+                if c in busy or topo.chip(c) != topo.chip(home):
+                    continue
+                if (topo.die(c) == topo.die(home)) != same_die:
+                    continue
+                if topo.may_write(c, dst) and all(topo.may_write(f, c) for f in feeders):
+                    busy.add(c)
+                    return c
+        return None
+
+    for r in range(n):
+        dst, near, far = cores[r], cores[(r - 1) % n], cores[(r - 2) % n]
+        barred = [s for s in (far, near) if not topo.may_write(s, dst)]
+        if len(barred) == 2:
+            h = relay(near, [far, near], dst)
+            job(first, far, ("pb",), h, 0)
+            job(first, near, ("pb",), h, 1)
+            job(first, h, ("in0", "in1"), dst, 1)
+        elif len(barred) == 1:
+            s = barred[0]
+            h = relay(s, [s], dst)
+            job(first, s, ("pb",), h, 0)
+            job(first, h, ("in0",), dst, 1)
+            job(then, far if s == near else near, ("pb",), dst, 0)
+        else:
+            job(then, far, ("pb",), dst, 0)
+            job(then, near, ("pb",), dst, 1)
+    return first, then, slots
+
+
+def _send(g, core, T, topo, first, then):
+    sent = 0
+    urgent = first.get(core, [])
+    taken = 0
+    transfers = []
+    for bufs, dst, slot in urgent:
+        rid, pid, _ = topo.addr(dst)
+        m = _engines(topo.mask(core, dst), NE, taken)
+        taken |= m
+        sent += NE
+        if len(urgent) == 1 and len(bufs) == 1:
+            g.remote_dma(out_ap=T["in%d" % slot][:], in_ap=T[bufs[0]][:], remote_sem=T.sem["arr%d" % slot],
+                         local_sem=T.sem.sent, pid=pid, routing_id=rid, dma_engine_mask=m)
+        elif len(bufs) == 1:
+            transfers.append(RemoteDMATransfer(dst_ids=[DstId(rid=rid, pnc=pid)], dma_engine_mask=m,
+                                               remote_sem=T.sem["arr%d" % slot], src=T[bufs[0]][:],
+                                               dst=T["in%d" % slot][:]))
+        else:
+            transfers.append(RemoteDMATransfer(dst_ids=[DstId(rid=rid, pnc=pid)], dma_engine_mask=m,
+                                               remote_sem=T.sem["arr%d" % slot], srcs=[T[b][:] for b in bufs],
+                                               dsts=[T["in%d" % slot][:]], alu_op=1))
+    if transfers:
+        g.remote_dma_fused(transfers, local_sem=T.sem.sent)
+    for bufs, dst, slot in then.get(core, []):
+        rid, pid, _ = topo.addr(dst)
+        g.remote_dma(out_ap=T["in%d" % slot][:], in_ap=T[bufs[0]][:], remote_sem=T.sem["arr%d" % slot],
+                     local_sem=T.sem.sent, pid=pid, routing_id=rid,
+                     dma_engine_mask=_engines(topo.mask(core, dst), NE))
+        sent += NE
+    return sent
+
+
+def rank_program(g, core, T, topo):
+    first, then, slots = _plan(T, topo)
+    rank = T.rank_of(core)
+
+    if rank is None:
+        if core not in first:
+            return
+        for slot in sorted(slots[core]):
+            g.wait_ge(T.sem["arr%d" % slot], NE)
+        g.wait_ge(T.sem.sent, _send(g, core, T, topo, first, then))
+        return
+
+    g.sync.dma_start(T.wsb[:], T.w[:]).then_inc(T.sem.loaded, 16)
+    g.scalar.dma_start(T.asb[:], T.a[:]).then_inc(T.sem.loaded, 16)
+    g.tensor.wait_ge(T.sem.loaded, 32)
+    g.tensor.matmul(T.ps[:], T.asb[:], T.wsb[:], True, True).then_inc(T.sem.mm, 1)
+    g.vector.wait_ge(T.sem.mm, 1)
+    g.vector.tensor_copy(T.pb[:], T.ps[:]).then_inc(T.sem.cp, 1)
+
+    g.wait_ge(T.sem.cp, 1)
+    sent = _send(g, core, T, topo, first, then)
+
+    base = T.ps
+    if 0 in slots[core]:
+        g.vector.wait_ge(T.sem.arr0, NE)
+        g.vector.tensor_tensor(T.acc[:], T.ps[:], T.in0[:], AluOpType.add).then_inc(T.sem.vs, 1)
+        g.vector.wait_ge(T.sem.vs, 1)
+        base = T.acc
+    g.vector.wait_ge(T.sem.arr1, NE)
+    g.vector.tensor_tensor(T.out[:], base[:], T.in1[:], AluOpType.add).then_inc(T.sem.fin, 1)
+
+    g.sync.wait_ge(T.sem.fin, 1)
+    g.sync.dma_start(T.y[:], T.out[:]).then_inc(T.sem.stored, 16)
+    g.sync.wait_ge(T.sem.stored, 16)
+    g.wait_ge(T.sem.sent, sent)

@@ -2,29 +2,32 @@ from concourse.bass import DstId, RemoteDMATransfer
 from concourse.mybir import AluOpType
 
 F = 512
-NE = 8
+H = F // 2
+HALVES = ((0, H), (H, F))
+K = 8
 
 SCRATCH = {
     "asb": ("sbuf", [128, 128], "bfloat16"),
     "wsb": ("sbuf", [128, F], "bfloat16"),
-    "ps": ("psum", [128, F], "float32"),
+    "ps0": ("psum", [128, F], "float32"),
+    "ps1": ("psum", [128, F], "float32"),
     "acc": ("psum", [128, F], "float32"),
     "pb": ("sbuf", [128, F], "bfloat16"),
     "in0": ("sbuf", [128, F], "bfloat16"),
     "in1": ("sbuf", [128, F], "bfloat16"),
     "out": ("sbuf", [128, F], "bfloat16"),
 }
-SEMAPHORES = ["loaded", "mm", "cp", "arr0", "arr1", "vs", "fin", "stored", "sent"]
+SEMAPHORES = ["ld0", "ld1", "mm0", "mm1", "cp0", "cp1", "arr0_0", "arr0_1", "arr1_0", "arr1_1", "vs", "fin0", "fin1",
+              "stored", "sent"]
+
+
+def _count(mask):
+    return sum((mask >> b) & 1 for b in range(mask.bit_length()))
 
 
 def _engines(mask, k, avoid=0):
-    got, n = 0, 0
-    for b in reversed(range(mask.bit_length())):
-        bit = 1 << b
-        if (mask & bit) and not (avoid & bit) and n < k:
-            got |= bit
-            n += 1
-    return got
+    bits = [1 << b for b in reversed(range(mask.bit_length())) if (mask >> b) & 1 and not (avoid >> b) & 1]
+    return sum(bits[:k])
 
 
 def _plan(T, topo):
@@ -33,106 +36,117 @@ def _plan(T, topo):
     busy = set(cores)
     first, then, slots = {}, {}, {}
 
-    def job(book, src, bufs, dst, slot):
-        book.setdefault(src, []).append((bufs, dst, slot))
-        slots.setdefault(dst, []).append(slot)
+    def job(book, src, buf, dst, slot):
+        book.setdefault(src, []).append((buf, dst, slot))
 
-    def relay(home, feeders, dst):
+    def relay(home, dst):
         for same_die in (True, False):
             for c in range(topo.CORES_PER_CHIP * topo.CHIPS):
-                if c in busy or topo.chip(c) != topo.chip(home):
+                if c in busy or topo.chip(c) != topo.chip(home) or (topo.die(c) == topo.die(home)) != same_die:
                     continue
-                if (topo.die(c) == topo.die(home)) != same_die:
-                    continue
-                if topo.may_write(c, dst) and all(topo.may_write(f, c) for f in feeders):
+                if topo.may_write(c, dst) and topo.may_write(home, c):
                     busy.add(c)
                     return c
         return None
 
     for r in range(n):
-        dst, near, far = cores[r], cores[(r - 1) % n], cores[(r - 2) % n]
-        barred = [s for s in (far, near) if not topo.may_write(s, dst)]
-        if len(barred) == 2:
-            h = relay(near, [far, near], dst)
-            job(first, far, ("pb",), h, 0)
-            job(first, near, ("pb",), h, 1)
-            job(first, h, ("in0", "in1"), dst, 1)
-        elif len(barred) == 1:
-            s = barred[0]
-            h = relay(s, [s], dst)
-            job(first, s, ("pb",), h, 0)
-            job(first, h, ("in0",), dst, 1)
-            job(then, far if s == near else near, ("pb",), dst, 0)
-        else:
-            job(then, far, ("pb",), dst, 0)
-            job(then, near, ("pb",), dst, 1)
+        dst = cores[r]
+        sources = [cores[(r - 2) % n], cores[(r - 1) % n]]
+        sources.sort(key=lambda s: not topo.may_write(s, dst))
+        for slot, s in enumerate(sources):
+            if topo.may_write(s, dst):
+                job(then, s, "pb", dst, slot)
+            else:
+                h = relay(s, dst)
+                job(first, s, "pb", h, 0)
+                job(first, h, "in0", dst, slot)
+
+    for book in (first, then):
+        for src in book:
+            taken, done = 0, []
+            for buf, dst, slot in book[src]:
+                allowed = topo.mask(src, dst)
+                if book is first:
+                    m = _engines(allowed, min(K, _count(allowed) // len(book[src])), taken)
+                    taken |= m
+                else:
+                    m = _engines(allowed, min(K, _count(allowed)))
+                done.append((buf, dst, slot, m))
+                slots.setdefault(dst, {})[slot] = (_count(m), len(HALVES) if book is first else 1)
+            book[src] = done
     return first, then, slots
 
 
-def _send(g, core, T, topo, first, then):
-    sent = 0
-    urgent = first.get(core, [])
-    taken = 0
-    transfers = []
-    for bufs, dst, slot in urgent:
+def _call(g, T, topo, jobs, lo, hi, piece):
+    transfers, n = [], 0
+    for buf, dst, slot, m in jobs:
         rid, pid, _ = topo.addr(dst)
-        m = _engines(topo.mask(core, dst), NE, taken)
-        taken |= m
-        sent += NE
-        if len(urgent) == 1 and len(bufs) == 1:
-            g.remote_dma(out_ap=T["in%d" % slot][:], in_ap=T[bufs[0]][:], remote_sem=T.sem["arr%d" % slot],
-                         local_sem=T.sem.sent, pid=pid, routing_id=rid, dma_engine_mask=m)
-        elif len(bufs) == 1:
-            transfers.append(RemoteDMATransfer(dst_ids=[DstId(rid=rid, pnc=pid)], dma_engine_mask=m,
-                                               remote_sem=T.sem["arr%d" % slot], src=T[bufs[0]][:],
-                                               dst=T["in%d" % slot][:]))
+        sem = T.sem["arr%d_%d" % (slot, piece)]
+        land = T["in%d" % slot][:, lo:hi]
+        n += _count(m)
+        if len(jobs) == 1:
+            g.remote_dma(out_ap=land, in_ap=T[buf][:, lo:hi], remote_sem=sem, local_sem=T.sem.sent, pid=pid,
+                         routing_id=rid, dma_engine_mask=m)
         else:
-            transfers.append(RemoteDMATransfer(dst_ids=[DstId(rid=rid, pnc=pid)], dma_engine_mask=m,
-                                               remote_sem=T.sem["arr%d" % slot], srcs=[T[b][:] for b in bufs],
-                                               dsts=[T["in%d" % slot][:]], alu_op=1))
+            transfers.append(RemoteDMATransfer(dst_ids=[DstId(rid=rid, pnc=pid)], dma_engine_mask=m, remote_sem=sem,
+                                               src=T[buf][:, lo:hi], dst=land))
     if transfers:
         g.remote_dma_fused(transfers, local_sem=T.sem.sent)
-    for bufs, dst, slot in then.get(core, []):
-        rid, pid, _ = topo.addr(dst)
-        g.remote_dma(out_ap=T["in%d" % slot][:], in_ap=T[bufs[0]][:], remote_sem=T.sem["arr%d" % slot],
-                     local_sem=T.sem.sent, pid=pid, routing_id=rid,
-                     dma_engine_mask=_engines(topo.mask(core, dst), NE))
-        sent += NE
-    return sent
+    return n
 
 
 def rank_program(g, core, T, topo):
     first, then, slots = _plan(T, topo)
     rank = T.rank_of(core)
+    sent = 0
 
     if rank is None:
         if core not in first:
             return
-        for slot in sorted(slots[core]):
-            g.wait_ge(T.sem["arr%d" % slot], NE)
-        g.wait_ge(T.sem.sent, _send(g, core, T, topo, first, then))
+        for h, (lo, hi) in enumerate(HALVES):
+            g.wait_ge(T.sem["arr0_%d" % h], slots[core][0][0])
+            sent += _call(g, T, topo, first[core], lo, hi, h)
+        g.wait_ge(T.sem.sent, sent)
         return
 
-    g.sync.dma_start(T.wsb[:], T.w[:]).then_inc(T.sem.loaded, 16)
-    g.scalar.dma_start(T.asb[:], T.a[:]).then_inc(T.sem.loaded, 16)
-    g.tensor.wait_ge(T.sem.loaded, 32)
-    g.tensor.matmul(T.ps[:], T.asb[:], T.wsb[:], True, True).then_inc(T.sem.mm, 1)
-    g.vector.wait_ge(T.sem.mm, 1)
-    g.vector.tensor_copy(T.pb[:], T.ps[:]).then_inc(T.sem.cp, 1)
+    g.sync.dma_start(T.wsb[:, 0:H], T.w[:, 0:H]).then_inc(T.sem.ld0, 16)
+    g.scalar.dma_start(T.asb[:], T.a[:]).then_inc(T.sem.ld0, 16)
+    g.scalar.dma_start(T.wsb[:, H:F], T.w[:, H:F]).then_inc(T.sem.ld1, 16)
+    for h, (lo, hi) in enumerate(HALVES):
+        g.tensor.wait_ge(T.sem["ld%d" % h], 16 if h else 32)
+        g.tensor.matmul(T["ps%d" % h][:, 0:H], T.asb[:], T.wsb[:, lo:hi], True, True).then_inc(T.sem["mm%d" % h], 1)
+    for h, (lo, hi) in enumerate(HALVES):
+        g.vector.wait_ge(T.sem["mm%d" % h], 1)
+        g.vector.tensor_copy(T.pb[:, lo:hi], T["ps%d" % h][:, 0:H]).then_inc(T.sem["cp%d" % h], 1)
 
-    g.wait_ge(T.sem.cp, 1)
-    sent = _send(g, core, T, topo, first, then)
+    for h, (lo, hi) in enumerate(HALVES):
+        g.wait_ge(T.sem["cp%d" % h], 1)
+        if core in first:
+            sent += _call(g, T, topo, first[core], lo, hi, h)
+    for j in then.get(core, []):
+        sent += _call(g, T, topo, [j], 0, F, 0)
 
-    base = T.ps
-    if 0 in slots[core]:
-        g.vector.wait_ge(T.sem.arr0, NE)
-        g.vector.tensor_tensor(T.acc[:], T.ps[:], T.in0[:], AluOpType.add).then_inc(T.sem.vs, 1)
-        g.vector.wait_ge(T.sem.vs, 1)
-        base = T.acc
-    g.vector.wait_ge(T.sem.arr1, NE)
-    g.vector.tensor_tensor(T.out[:], base[:], T.in1[:], AluOpType.add).then_inc(T.sem.fin, 1)
+    count0, pieces0 = slots[core][0]
+    count1, pieces1 = slots[core][1]
+    if pieces0 == 1:
+        g.vector.wait_ge(T.sem.arr0_0, count0)
+        for h, (lo, hi) in enumerate(HALVES):
+            g.vector.tensor_tensor(T.acc[:, lo:hi], T["ps%d" % h][:, 0:H], T.in0[:, lo:hi],
+                                   AluOpType.add).then_inc(T.sem.vs, 1)
+        g.vector.wait_ge(T.sem.vs, len(HALVES))
+    spans = HALVES if pieces1 > 1 else ((0, F),)
+    for i, (lo, hi) in enumerate(spans):
+        if pieces0 > 1:
+            g.vector.wait_ge(T.sem["arr0_%d" % i], count0)
+            g.vector.tensor_tensor(T.acc[:, lo:hi], T["ps%d" % i][:, 0:H], T.in0[:, lo:hi],
+                                   AluOpType.add).then_inc(T.sem.vs, 1)
+            g.vector.wait_ge(T.sem.vs, i + 1)
+        g.vector.wait_ge(T.sem["arr1_%d" % i], count1)
+        g.vector.tensor_tensor(T.out[:, lo:hi], T.acc[:, lo:hi], T.in1[:, lo:hi],
+                               AluOpType.add).then_inc(T.sem["fin%d" % i], 1)
+        q = g.sync if i == len(spans) - 1 else g.scalar
+        q.wait_ge(T.sem["fin%d" % i], 1)
+        q.dma_start(T.y[:, lo:hi], T.out[:, lo:hi]).then_inc(T.sem.stored, 16)
 
-    g.sync.wait_ge(T.sem.fin, 1)
-    g.sync.dma_start(T.y[:], T.out[:]).then_inc(T.sem.stored, 16)
-    g.sync.wait_ge(T.sem.stored, 16)
+    g.wait_ge(T.sem.stored, 16 * len(spans))
     g.wait_ge(T.sem.sent, sent)

@@ -1,24 +1,25 @@
 from concourse.bass import DstId, RemoteDMATransfer
-from concourse.mybir import AluOpType
 
 F = 512
 H = F // 2
 HALVES = ((0, H), (H, F))
+BAND = 2
 K = 8
 
 SCRATCH = {
-    "asb": ("sbuf", [128, 128], "bfloat16"),
-    "wsb": ("sbuf", [128, F], "bfloat16"),
+    "ad": ("dram", [128, 128], "bfloat16"),
+    "wd": ("dram", [128, F], "bfloat16"),
+    "a0": ("sbuf", [128, 128], "bfloat16"),
+    "w0": ("sbuf", [128, F], "bfloat16"),
+    "a1": ("sbuf", [128, 128], "bfloat16"),
+    "w1": ("sbuf", [128, F], "bfloat16"),
+    "a2": ("sbuf", [128, 128], "bfloat16"),
+    "w2": ("sbuf", [128, F], "bfloat16"),
     "ps0": ("psum", [128, F], "float32"),
     "ps1": ("psum", [128, F], "float32"),
-    "acc": ("psum", [128, F], "float32"),
-    "pb": ("sbuf", [128, F], "bfloat16"),
-    "in0": ("sbuf", [128, F], "bfloat16"),
-    "in1": ("sbuf", [128, F], "bfloat16"),
     "out": ("sbuf", [128, F], "bfloat16"),
 }
-SEMAPHORES = ["ld0", "ld1", "mm0", "mm1", "cp0", "cp1", "arr0_0", "arr0_1", "arr1_0", "arr1_1", "vs", "fin0", "fin1",
-              "stored", "sent"]
+SEMAPHORES = ["ca", "cw", "ld", "ra", "rw", "sa0", "sw0", "sa1", "sw1", "mm0", "mm1", "fin0", "fin1", "stored", "sent"]
 
 
 def _count(mask):
@@ -34,119 +35,130 @@ def _plan(T, topo):
     cores = list(T.cores)
     n = len(cores)
     busy = set(cores)
-    first, then, slots = {}, {}, {}
+    load = {}
 
-    def job(book, src, buf, dst, slot):
-        book.setdefault(src, []).append((buf, dst, slot))
+    def ports(c, dst):
+        a, b, d = topo.chip(c), topo.chip(dst), topo.die(c)
+        return ((a, d, "out", topo.same_plane(a, b)), (b, d, "in", topo.mates(a, b)))
+
+    def book(c, dst):
+        for p in ports(c, dst):
+            load[p] = load.get(p, 0) + 1
+
+    straight = {}
+    for j, s in enumerate(cores):
+        used = False
+        for k in range(1, BAND + 1):
+            dst = cores[(j + k) % n]
+            straight[(s, dst)] = topo.may_write(s, dst) and not used
+            if straight[(s, dst)]:
+                used = True
+                book(s, dst)
 
     def relay(home, dst):
-        for same_die in (True, False):
-            for c in range(topo.CORES_PER_CHIP * topo.CHIPS):
-                if c in busy or topo.chip(c) != topo.chip(home) or (topo.die(c) == topo.die(home)) != same_die:
-                    continue
-                if topo.may_write(c, dst) and topo.may_write(home, c):
-                    busy.add(c)
-                    return c
-        return None
+        best = None
+        for c in range(topo.CORES_PER_CHIP * topo.CHIPS):
+            if c in busy or topo.chip(c) != topo.chip(home):
+                continue
+            if not (topo.may_write(c, dst) and topo.may_write(home, c)):
+                continue
+            key = (sum(load.get(p, 0) for p in ports(c, dst)), topo.die(c) != topo.die(home), c)
+            if best is None or key < best:
+                best = key
+        busy.add(best[2])
+        book(best[2], dst)
+        return best[2]
 
+    feeds, onward, direct, counts = {}, {}, {}, {}
     for r in range(n):
         dst = cores[r]
-        sources = [cores[(r - 2) % n], cores[(r - 1) % n]]
-        sources.sort(key=lambda s: not topo.may_write(s, dst))
+        sources = [cores[(r - k) % n] for k in range(BAND, 0, -1)]
+        sources.sort(key=lambda s: not straight[(s, dst)])
         for slot, s in enumerate(sources):
-            if topo.may_write(s, dst):
-                job(then, s, "pb", dst, slot)
+            c = s if straight[(s, dst)] else relay(s, dst)
+            m = _engines(topo.mask(c, dst), K)
+            counts.setdefault(dst, {})[slot] = _count(m)
+            if c == s:
+                direct[s] = (dst, slot, m)
             else:
-                h = relay(s, dst)
-                job(first, s, "pb", h, 0)
-                job(first, h, "in0", dst, slot)
-
-    for book in (first, then):
-        for src in book:
-            taken, done = 0, []
-            for buf, dst, slot in book[src]:
-                allowed = topo.mask(src, dst)
-                if book is first:
-                    m = _engines(allowed, min(K, _count(allowed) // len(book[src])), taken)
-                    taken |= m
-                else:
-                    m = _engines(allowed, min(K, _count(allowed)))
-                done.append((buf, dst, slot, m))
-                slots.setdefault(dst, {})[slot] = (_count(m), len(HALVES) if book is first else 1)
-            book[src] = done
-    return first, then, slots
+                feeds.setdefault(s, []).append(c)
+                onward[c] = (dst, slot, m)
+    for s in feeds:
+        taken, done = 0, []
+        for c in feeds[s]:
+            allowed = topo.mask(s, c)
+            m = _engines(allowed, min(K, _count(allowed) // len(feeds[s])), taken)
+            taken |= m
+            done.append((c, m))
+        feeds[s] = done
+    return feeds, onward, direct, counts
 
 
-def _call(g, T, topo, jobs, lo, hi, piece):
+def _send(g, T, topo, jobs, src, land, sem):
     transfers, n = [], 0
-    for buf, dst, slot, m in jobs:
+    for dst, m in jobs:
         rid, pid, _ = topo.addr(dst)
-        sem = T.sem["arr%d_%d" % (slot, piece)]
-        land = T["in%d" % slot][:, lo:hi]
         n += _count(m)
         if len(jobs) == 1:
-            g.remote_dma(out_ap=land, in_ap=T[buf][:, lo:hi], remote_sem=sem, local_sem=T.sem.sent, pid=pid,
+            g.remote_dma(out_ap=T[land][:], in_ap=T[src][:], remote_sem=T.sem[sem], local_sem=T.sem.sent, pid=pid,
                          routing_id=rid, dma_engine_mask=m)
         else:
-            transfers.append(RemoteDMATransfer(dst_ids=[DstId(rid=rid, pnc=pid)], dma_engine_mask=m, remote_sem=sem,
-                                               src=T[buf][:, lo:hi], dst=land))
+            transfers.append(RemoteDMATransfer(dst_ids=[DstId(rid=rid, pnc=pid)], dma_engine_mask=m,
+                                               remote_sem=T.sem[sem], src=T[src][:], dst=T[land][:]))
     if transfers:
         g.remote_dma_fused(transfers, local_sem=T.sem.sent)
     return n
 
 
 def rank_program(g, core, T, topo):
-    first, then, slots = _plan(T, topo)
+    feeds, onward, direct, counts = _plan(T, topo)
     rank = T.rank_of(core)
     sent = 0
 
     if rank is None:
-        if core not in first:
+        if core not in onward:
             return
-        for h, (lo, hi) in enumerate(HALVES):
-            g.wait_ge(T.sem["arr0_%d" % h], slots[core][0][0])
-            sent += _call(g, T, topo, first[core], lo, hi, h)
+        dst, slot, m = onward[core]
+        fed = [k for s in feeds for c, k in feeds[s] if c == core][0]
+        for x in "aw":
+            g.wait_ge(T.sem["r" + x], _count(fed))
+            sent += _send(g, T, topo, [(dst, m)], x + "d", "%s%d" % (x, slot + 1), "s%s%d" % (x, slot))
         g.wait_ge(T.sem.sent, sent)
         return
 
-    g.sync.dma_start(T.wsb[:, 0:H], T.w[:, 0:H]).then_inc(T.sem.ld0, 16)
-    g.scalar.dma_start(T.asb[:], T.a[:]).then_inc(T.sem.ld0, 16)
-    g.scalar.dma_start(T.wsb[:, H:F], T.w[:, H:F]).then_inc(T.sem.ld1, 16)
-    for h, (lo, hi) in enumerate(HALVES):
-        g.tensor.wait_ge(T.sem["ld%d" % h], 16 if h else 32)
-        g.tensor.matmul(T["ps%d" % h][:, 0:H], T.asb[:], T.wsb[:, lo:hi], True, True).then_inc(T.sem["mm%d" % h], 1)
+    g.sync.dma_start(T.ad[:], T.a[:]).then_inc(T.sem.ca, 16)
+    g.sync.dma_start(T.wd[:], T.w[:]).then_inc(T.sem.cw, 16)
+    g.scalar.wait_ge(T.sem.ca, 16)
+    g.scalar.dma_start(T.a0[:], T.a[:]).then_inc(T.sem.ld, 16)
+    g.scalar.dma_start(T.w0[:], T.w[:]).then_inc(T.sem.ld, 16)
+
+    for x in "aw":
+        g.wait_ge(T.sem["c" + x], 16)
+        if core in feeds:
+            sent += _send(g, T, topo, feeds[core], x + "d", x + "d", "r" + x)
+    if core in direct:
+        dst, slot, m = direct[core]
+        for x in "aw":
+            sent += _send(g, T, topo, [(dst, m)], x + "d", "%s%d" % (x, slot + 1), "s%s%d" % (x, slot))
+
+    last = len(counts[core])
+    for k in range(last + 1):
+        if k == 0:
+            g.tensor.wait_ge(T.sem.ld, 32)
+        else:
+            g.tensor.wait_ge(T.sem["sa%d" % (k - 1)], counts[core][k - 1])
+            g.tensor.wait_ge(T.sem["sw%d" % (k - 1)], counts[core][k - 1])
+        for h, (lo, hi) in enumerate(HALVES):
+            mm = g.tensor.matmul(T["ps%d" % h][:, 0:H], T["a%d" % k][:], T["w%d" % k][:, lo:hi], k == 0, k == last)
+            if k == last:
+                mm.then_inc(T.sem["mm%d" % h], 1)
+
     for h, (lo, hi) in enumerate(HALVES):
         g.vector.wait_ge(T.sem["mm%d" % h], 1)
-        g.vector.tensor_copy(T.pb[:, lo:hi], T["ps%d" % h][:, 0:H]).then_inc(T.sem["cp%d" % h], 1)
-
-    for h, (lo, hi) in enumerate(HALVES):
-        g.wait_ge(T.sem["cp%d" % h], 1)
-        if core in first:
-            sent += _call(g, T, topo, first[core], lo, hi, h)
-    for j in then.get(core, []):
-        sent += _call(g, T, topo, [j], 0, F, 0)
-
-    count0, pieces0 = slots[core][0]
-    count1, pieces1 = slots[core][1]
-    if pieces0 == 1:
-        g.vector.wait_ge(T.sem.arr0_0, count0)
-        for h, (lo, hi) in enumerate(HALVES):
-            g.vector.tensor_tensor(T.acc[:, lo:hi], T["ps%d" % h][:, 0:H], T.in0[:, lo:hi],
-                                   AluOpType.add).then_inc(T.sem.vs, 1)
-        g.vector.wait_ge(T.sem.vs, len(HALVES))
-    spans = HALVES if pieces1 > 1 else ((0, F),)
-    for i, (lo, hi) in enumerate(spans):
-        if pieces0 > 1:
-            g.vector.wait_ge(T.sem["arr0_%d" % i], count0)
-            g.vector.tensor_tensor(T.acc[:, lo:hi], T["ps%d" % i][:, 0:H], T.in0[:, lo:hi],
-                                   AluOpType.add).then_inc(T.sem.vs, 1)
-            g.vector.wait_ge(T.sem.vs, i + 1)
-        g.vector.wait_ge(T.sem["arr1_%d" % i], count1)
-        g.vector.tensor_tensor(T.out[:, lo:hi], T.acc[:, lo:hi], T.in1[:, lo:hi],
-                               AluOpType.add).then_inc(T.sem["fin%d" % i], 1)
-        q = g.sync if i == len(spans) - 1 else g.scalar
-        q.wait_ge(T.sem["fin%d" % i], 1)
+        g.vector.tensor_copy(T.out[:, lo:hi], T["ps%d" % h][:, 0:H]).then_inc(T.sem["fin%d" % h], 1)
+        q = g.sync if h == len(HALVES) - 1 else g.scalar
+        q.wait_ge(T.sem["fin%d" % h], 1)
         q.dma_start(T.y[:, lo:hi], T.out[:, lo:hi]).then_inc(T.sem.stored, 16)
 
-    g.wait_ge(T.sem.stored, 16 * len(spans))
+    g.wait_ge(T.sem.stored, 16 * len(HALVES))
     g.wait_ge(T.sem.sent, sent)

@@ -1,25 +1,32 @@
 from concourse.bass import DstId, RemoteDMATransfer
+from concourse.mybir import AluOpType, ActivationFunctionType
 
 F = 512
-H = F // 2
-HALVES = ((0, H), (H, F))
+X = 320
+R = F - X
 BAND = 2
 K = 8
+PIECES = ("a", "l", "p")
+SRC = {"a": "ad", "l": "wl", "p": "pr"}
 
 SCRATCH = {
     "ad": ("dram", [128, 128], "bfloat16"),
-    "wd": ("dram", [128, F], "bfloat16"),
+    "wl": ("dram", [128, X], "bfloat16"),
+    "pr": ("sbuf", [128, R], "bfloat16"),
     "a0": ("sbuf", [128, 128], "bfloat16"),
     "w0": ("sbuf", [128, F], "bfloat16"),
     "a1": ("sbuf", [128, 128], "bfloat16"),
-    "w1": ("sbuf", [128, F], "bfloat16"),
+    "l1": ("sbuf", [128, X], "bfloat16"),
+    "p1": ("sbuf", [128, R], "bfloat16"),
     "a2": ("sbuf", [128, 128], "bfloat16"),
-    "w2": ("sbuf", [128, F], "bfloat16"),
-    "ps0": ("psum", [128, F], "float32"),
-    "ps1": ("psum", [128, F], "float32"),
+    "l2": ("sbuf", [128, X], "bfloat16"),
+    "p2": ("sbuf", [128, R], "bfloat16"),
+    "psl": ("psum", [128, F], "float32"),
+    "psr": ("psum", [128, F], "float32"),
     "out": ("sbuf", [128, F], "bfloat16"),
 }
-SEMAPHORES = ["ca", "cw", "ld", "ra", "rw", "sa0", "sw0", "sa1", "sw1", "mm0", "mm1", "fin0", "fin1", "stored", "sent"]
+SEMAPHORES = ["ca", "cl", "ldr", "ldl", "pm", "pv", "ra", "rl", "rp", "sa0", "sl0", "sp0", "sa1", "sl1", "sp1",
+              "mml", "acc", "finl", "finr", "stored", "sent"]
 
 
 def _count(mask):
@@ -29,6 +36,11 @@ def _count(mask):
 def _engines(mask, k, avoid=0):
     bits = [1 << b for b in reversed(range(mask.bit_length())) if (mask >> b) & 1 and not (avoid >> b) & 1]
     return sum(bits[:k])
+
+
+def _spread(mask, k):
+    bits = [1 << b for b in range(mask.bit_length()) if (mask >> b) & 1]
+    return sum(bits[::max(1, len(bits) // k)][:k])
 
 
 def _plan(T, topo):
@@ -94,6 +106,10 @@ def _plan(T, topo):
     return feeds, onward, direct, counts
 
 
+def _feed_mask(x, m):
+    return _spread(m, _count(m) // 2) if x == "a" else m
+
+
 def _send(g, T, topo, jobs, src, land, sem):
     transfers, n = [], 0
     for dst, m in jobs:
@@ -120,45 +136,58 @@ def rank_program(g, core, T, topo):
             return
         dst, slot, m = onward[core]
         fed = [k for s in feeds for c, k in feeds[s] if c == core][0]
-        for x in "aw":
-            g.wait_ge(T.sem["r" + x], _count(fed))
-            sent += _send(g, T, topo, [(dst, m)], x + "d", "%s%d" % (x, slot + 1), "s%s%d" % (x, slot))
+        for x in PIECES:
+            g.wait_ge(T.sem["r" + x], _count(_feed_mask(x, fed)))
+            sent += _send(g, T, topo, [(dst, m)], SRC[x], "%s%d" % (x, slot + 1), "s%s%d" % (x, slot))
         g.wait_ge(T.sem.sent, sent)
         return
 
     g.sync.dma_start(T.ad[:], T.a[:]).then_inc(T.sem.ca, 16)
-    g.sync.dma_start(T.wd[:], T.w[:]).then_inc(T.sem.cw, 16)
-    g.scalar.wait_ge(T.sem.ca, 16)
-    g.scalar.dma_start(T.a0[:], T.a[:]).then_inc(T.sem.ld, 16)
-    g.scalar.dma_start(T.w0[:], T.w[:]).then_inc(T.sem.ld, 16)
+    g.sync.dma_start(T.wl[:], T.w[:, 0:X]).then_inc(T.sem.cl, 16)
+    g.scalar.dma_start(T.a0[:], T.a[:]).then_inc(T.sem.ldr, 16)
+    g.scalar.dma_start(T.w0[:, X:F], T.w[:, X:F]).then_inc(T.sem.ldr, 16)
+    g.scalar.dma_start(T.w0[:, 0:X], T.w[:, 0:X]).then_inc(T.sem.ldl, 16)
 
-    for x in "aw":
-        g.wait_ge(T.sem["c" + x], 16)
-        if core in feeds:
-            sent += _send(g, T, topo, feeds[core], x + "d", x + "d", "r" + x)
-    if core in direct:
-        dst, slot, m = direct[core]
-        for x in "aw":
-            sent += _send(g, T, topo, [(dst, m)], x + "d", "%s%d" % (x, slot + 1), "s%s%d" % (x, slot))
+    ready = {"a": ("ca", 16), "l": ("cl", 16), "p": ("pv", 1)}
+    for group in (PIECES[:2], PIECES[2:]):
+        for x in group:
+            g.wait_ge(T.sem[ready[x][0]], ready[x][1])
+            if core in feeds:
+                sent += _send(g, T, topo, [(c, _feed_mask(x, m)) for c, m in feeds[core]], SRC[x], SRC[x], "r" + x)
+        if core in direct:
+            dst, slot, m = direct[core]
+            for x in group:
+                sent += _send(g, T, topo, [(dst, m)], SRC[x], "%s%d" % (x, slot + 1), "s%s%d" % (x, slot))
 
     last = len(counts[core])
-    for k in range(last + 1):
-        if k == 0:
-            g.tensor.wait_ge(T.sem.ld, 32)
+    g.tensor.wait_ge(T.sem.ldr, 32)
+    g.tensor.matmul(T.psr[:, 0:R], T.a0[:], T.w0[:, X:F], True, True).then_inc(T.sem.pm, 1)
+    g.tensor.wait_ge(T.sem.ldl, 16)
+    g.tensor.matmul(T.psl[:, 0:X], T.a0[:], T.w0[:, 0:X], True, False)
+    for k in range(1, last + 1):
+        g.tensor.wait_ge(T.sem["sa%d" % (k - 1)], counts[core][k - 1])
+        g.tensor.wait_ge(T.sem["sl%d" % (k - 1)], counts[core][k - 1])
+        mm = g.tensor.matmul(T.psl[:, 0:X], T["a%d" % k][:], T["l%d" % k][:], False, k == last)
+        if k == last:
+            mm.then_inc(T.sem.mml, 1)
+
+    g.vector.wait_ge(T.sem.pm, 1)
+    g.vector.tensor_copy(T.pr[:], T.psr[:, 0:R]).then_inc(T.sem.pv, 1)
+    g.vector.wait_ge(T.sem.pv, 1)
+    for k in range(1, last + 1):
+        g.vector.wait_ge(T.sem["sp%d" % (k - 1)], counts[core][k - 1])
+        if k < last:
+            g.vector.tensor_tensor(T.psr[:, 0:R], T.psr[:, 0:R], T["p%d" % k][:], AluOpType.add).then_inc(T.sem.acc, 1)
+            g.vector.wait_ge(T.sem.acc, k)
         else:
-            g.tensor.wait_ge(T.sem["sa%d" % (k - 1)], counts[core][k - 1])
-            g.tensor.wait_ge(T.sem["sw%d" % (k - 1)], counts[core][k - 1])
-        for h, (lo, hi) in enumerate(HALVES):
-            mm = g.tensor.matmul(T["ps%d" % h][:, 0:H], T["a%d" % k][:], T["w%d" % k][:, lo:hi], k == 0, k == last)
-            if k == last:
-                mm.then_inc(T.sem["mm%d" % h], 1)
+            g.vector.tensor_tensor(T.out[:, X:F], T.psr[:, 0:R], T["p%d" % k][:], AluOpType.add).then_inc(T.sem.finr, 1)
+    g.sync.wait_ge(T.sem.finr, 1)
+    g.sync.dma_start(T.y[:, X:F], T.out[:, X:F]).then_inc(T.sem.stored, 16)
 
-    for h, (lo, hi) in enumerate(HALVES):
-        g.vector.wait_ge(T.sem["mm%d" % h], 1)
-        g.vector.tensor_copy(T.out[:, lo:hi], T["ps%d" % h][:, 0:H]).then_inc(T.sem["fin%d" % h], 1)
-        q = g.sync if h == len(HALVES) - 1 else g.scalar
-        q.wait_ge(T.sem["fin%d" % h], 1)
-        q.dma_start(T.y[:, lo:hi], T.out[:, lo:hi]).then_inc(T.sem.stored, 16)
+    g.scalar.wait_ge(T.sem.mml, 1)
+    g.scalar.activation(T.out[:, 0:X], T.psl[:, 0:X], ActivationFunctionType.Copy).then_inc(T.sem.finl, 1)
+    g.scalar.wait_ge(T.sem.finl, 1)
+    g.scalar.dma_start(T.y[:, 0:X], T.out[:, 0:X]).then_inc(T.sem.stored, 16)
 
-    g.wait_ge(T.sem.stored, 16 * len(HALVES))
+    g.wait_ge(T.sem.stored, 32)
     g.wait_ge(T.sem.sent, sent)

from concourse.bass import DstId, RemoteDMATransfer
from concourse.mybir import AluOpType, ActivationFunctionType

F = 512
X = 320
R = F - X
BAND = 2
K = 8
PIECES = ("a", "l", "p")
SRC = {"a": "ad", "l": "wl", "p": "pr"}

SCRATCH = {
    "ad": ("dram", [128, 128], "bfloat16"),
    "wl": ("dram", [128, X], "bfloat16"),
    "pr": ("sbuf", [128, R], "bfloat16"),
    "a0": ("sbuf", [128, 128], "bfloat16"),
    "w0": ("sbuf", [128, F], "bfloat16"),
    "a1": ("sbuf", [128, 128], "bfloat16"),
    "l1": ("sbuf", [128, X], "bfloat16"),
    "p1": ("sbuf", [128, R], "bfloat16"),
    "a2": ("sbuf", [128, 128], "bfloat16"),
    "l2": ("sbuf", [128, X], "bfloat16"),
    "p2": ("sbuf", [128, R], "bfloat16"),
    "psl": ("psum", [128, F], "float32"),
    "psr": ("psum", [128, F], "float32"),
    "out": ("sbuf", [128, F], "bfloat16"),
}
SEMAPHORES = ["ca", "cl", "ldr", "ldl", "pm", "pv", "ra", "rl", "rp", "sa0", "sl0", "sp0", "sa1", "sl1", "sp1",
              "mml", "acc", "finl", "finr", "stored", "sent"]


def _count(mask):
    return sum((mask >> b) & 1 for b in range(mask.bit_length()))


def _engines(mask, k, avoid=0):
    bits = [1 << b for b in reversed(range(mask.bit_length())) if (mask >> b) & 1 and not (avoid >> b) & 1]
    return sum(bits[:k])


def _spread(mask, k):
    bits = [1 << b for b in range(mask.bit_length()) if (mask >> b) & 1]
    return sum(bits[::max(1, len(bits) // k)][:k])


def _plan(T, topo):
    cores = list(T.cores)
    n = len(cores)
    busy = set(cores)
    load = {}

    def ports(c, dst):
        a, b, d = topo.chip(c), topo.chip(dst), topo.die(c)
        return ((a, d, "out", topo.same_plane(a, b)), (b, d, "in", topo.mates(a, b)))

    def book(c, dst):
        for p in ports(c, dst):
            load[p] = load.get(p, 0) + 1

    straight = {}
    for j, s in enumerate(cores):
        used = False
        for k in range(1, BAND + 1):
            dst = cores[(j + k) % n]
            straight[(s, dst)] = topo.may_write(s, dst) and not used
            if straight[(s, dst)]:
                used = True
                book(s, dst)

    def relay(home, dst):
        best = None
        for c in range(topo.CORES_PER_CHIP * topo.CHIPS):
            if c in busy or topo.chip(c) != topo.chip(home):
                continue
            if not (topo.may_write(c, dst) and topo.may_write(home, c)):
                continue
            key = (sum(load.get(p, 0) for p in ports(c, dst)), topo.die(c) != topo.die(home), c)
            if best is None or key < best:
                best = key
        busy.add(best[2])
        book(best[2], dst)
        return best[2]

    feeds, onward, direct, counts = {}, {}, {}, {}
    for r in range(n):
        dst = cores[r]
        sources = [cores[(r - k) % n] for k in range(BAND, 0, -1)]
        sources.sort(key=lambda s: not straight[(s, dst)])
        for slot, s in enumerate(sources):
            c = s if straight[(s, dst)] else relay(s, dst)
            m = _engines(topo.mask(c, dst), K)
            counts.setdefault(dst, {})[slot] = _count(m)
            if c == s:
                direct[s] = (dst, slot, m)
            else:
                feeds.setdefault(s, []).append(c)
                onward[c] = (dst, slot, m)
    for s in feeds:
        taken, done = 0, []
        for c in feeds[s]:
            allowed = topo.mask(s, c)
            m = _engines(allowed, min(K, _count(allowed) // len(feeds[s])), taken)
            taken |= m
            done.append((c, m))
        feeds[s] = done
    return feeds, onward, direct, counts


def _feed_mask(x, m):
    return _spread(m, _count(m) // 2) if x == "a" else m


def _send(g, T, topo, jobs, src, land, sem):
    transfers, n = [], 0
    for dst, m in jobs:
        rid, pid, _ = topo.addr(dst)
        n += _count(m)
        if len(jobs) == 1:
            g.remote_dma(out_ap=T[land][:], in_ap=T[src][:], remote_sem=T.sem[sem], local_sem=T.sem.sent, pid=pid,
                         routing_id=rid, dma_engine_mask=m)
        else:
            transfers.append(RemoteDMATransfer(dst_ids=[DstId(rid=rid, pnc=pid)], dma_engine_mask=m,
                                               remote_sem=T.sem[sem], src=T[src][:], dst=T[land][:]))
    if transfers:
        g.remote_dma_fused(transfers, local_sem=T.sem.sent)
    return n


def rank_program(g, core, T, topo):
    feeds, onward, direct, counts = _plan(T, topo)
    rank = T.rank_of(core)
    sent = 0

    if rank is None:
        if core not in onward:
            return
        dst, slot, m = onward[core]
        fed = [k for s in feeds for c, k in feeds[s] if c == core][0]
        for x in PIECES:
            g.wait_ge(T.sem["r" + x], _count(_feed_mask(x, fed)))
            sent += _send(g, T, topo, [(dst, m)], SRC[x], "%s%d" % (x, slot + 1), "s%s%d" % (x, slot))
        g.wait_ge(T.sem.sent, sent)
        return

    g.sync.dma_start(T.ad[:], T.a[:]).then_inc(T.sem.ca, 16)
    g.sync.dma_start(T.wl[:], T.w[:, 0:X]).then_inc(T.sem.cl, 16)
    g.scalar.dma_start(T.a0[:], T.a[:]).then_inc(T.sem.ldr, 16)
    g.scalar.dma_start(T.w0[:, X:F], T.w[:, X:F]).then_inc(T.sem.ldr, 16)
    g.scalar.dma_start(T.w0[:, 0:X], T.w[:, 0:X]).then_inc(T.sem.ldl, 16)

    ready = {"a": ("ca", 16), "l": ("cl", 16), "p": ("pv", 1)}
    for group in (PIECES[:2], PIECES[2:]):
        for x in group:
            g.wait_ge(T.sem[ready[x][0]], ready[x][1])
            if core in feeds:
                sent += _send(g, T, topo, [(c, _feed_mask(x, m)) for c, m in feeds[core]], SRC[x], SRC[x], "r" + x)
        if core in direct:
            dst, slot, m = direct[core]
            for x in group:
                sent += _send(g, T, topo, [(dst, m)], SRC[x], "%s%d" % (x, slot + 1), "s%s%d" % (x, slot))

    last = len(counts[core])
    g.tensor.wait_ge(T.sem.ldr, 32)
    g.tensor.matmul(T.psr[:, 0:R], T.a0[:], T.w0[:, X:F], True, True).then_inc(T.sem.pm, 1)
    g.tensor.wait_ge(T.sem.ldl, 16)
    g.tensor.matmul(T.psl[:, 0:X], T.a0[:], T.w0[:, 0:X], True, False)
    for k in range(1, last + 1):
        g.tensor.wait_ge(T.sem["sa%d" % (k - 1)], counts[core][k - 1])
        g.tensor.wait_ge(T.sem["sl%d" % (k - 1)], counts[core][k - 1])
        mm = g.tensor.matmul(T.psl[:, 0:X], T["a%d" % k][:], T["l%d" % k][:], False, k == last)
        if k == last:
            mm.then_inc(T.sem.mml, 1)

    g.vector.wait_ge(T.sem.pm, 1)
    g.vector.tensor_copy(T.pr[:], T.psr[:, 0:R]).then_inc(T.sem.pv, 1)
    g.vector.wait_ge(T.sem.pv, 1)
    for k in range(1, last + 1):
        g.vector.wait_ge(T.sem["sp%d" % (k - 1)], counts[core][k - 1])
        if k < last:
            g.vector.tensor_tensor(T.psr[:, 0:R], T.psr[:, 0:R], T["p%d" % k][:], AluOpType.add).then_inc(T.sem.acc, 1)
            g.vector.wait_ge(T.sem.acc, k)
        else:
            g.vector.tensor_tensor(T.out[:, X:F], T.psr[:, 0:R], T["p%d" % k][:], AluOpType.add).then_inc(T.sem.finr, 1)
    g.sync.wait_ge(T.sem.finr, 1)
    g.sync.dma_start(T.y[:, X:F], T.out[:, X:F]).then_inc(T.sem.stored, 16)

    g.scalar.wait_ge(T.sem.mml, 1)
    g.scalar.activation(T.out[:, 0:X], T.psl[:, 0:X], ActivationFunctionType.Copy).then_inc(T.sem.finl, 1)
    g.scalar.wait_ge(T.sem.finl, 1)
    g.scalar.dma_start(T.y[:, 0:X], T.out[:, 0:X]).then_inc(T.sem.stored, 16)

    g.wait_ge(T.sem.stored, 32)
    g.wait_ge(T.sem.sent, sent)
